import numpy as np, ml_dtypes
CORES = [13,21,141,149]
N = 4
BF = ml_dtypes.bfloat16
W, L, OR, ST, NEED = 2048, 256, 4, 3, 9
def forest(rng):
    o = np.argsort(rng.random((N, 8, 16, L, OR)), axis=2); k = np.arange(16).reshape(1, 1, 16, 1, 1)
    q = (rng.random(o.shape) * k).astype(np.int64); p = np.zeros_like(o)
    np.put_along_axis(p, o, np.take_along_axis(o, q, 2), 2)
    return np.where(rng.random(p.shape) < 0.1, k, p)
def limits(rng, lo, n):
    base = np.argsort(rng.random((N, 8, 1, L)), axis=-1) % n + lo
    return np.clip(base + rng.integers(-2, 3, (N, 8, 16, L)), 0, 15)
def parts(rng):
    x = rng.integers(0, 16, (N, 8, 16, W)); c = rng.integers(0, W, (N, 8, 16, L, OR)); p = forest(rng); a = limits(rng, 3, 8)
    v = rng.integers(0, 33, (N, 8, OR, L))
    o = np.arange(OR).reshape(1, 1, OR, 1); fav = rng.integers(0, OR, (1, 8, 1, L)); stick = rng.random((1, 8, 1, L)) < 0.5
    v = np.where(stick, np.where(o == fav, rng.integers(20, 33, v.shape), rng.integers(0, 7, v.shape)), v)
    return x, c, p, a, v
def bf(a): return np.ascontiguousarray(a).astype(np.float32).astype(BF)
def pack(x, c, p, a, v):
    return {"xt": bf(x.reshape(N, 128, W)), "pg": np.ascontiguousarray(c.reshape(N, 128, L * OR)).astype(np.int32), "pre": bf(p.reshape(N, 128, L * OR)),
            "lim": bf(a.reshape(N, 128, L)), "vv": np.ascontiguousarray(v.reshape(N, 8 * OR, L)).astype(np.int32)}
def setup_inputs(rng):
    return pack(*parts(rng))
def setup_inputs_ties(rng):
    x, c, p, a, v = parts(rng)
    dl = rng.integers(1, 8, (1, 8, 1, 1)); x = rng.integers(0, 9, (N, 8, 16, 1)) + dl * rng.integers(0, 2, x.shape)
    k = np.argsort(rng.random((N, 8, 1, L)), axis=-1) % 5; n = np.array([0, 2 * NEED - 16, 2 * NEED - 15, NEED - 1, 16])[k]
    a = np.where(np.argsort(rng.random(a.shape), axis=2) < n, dl, dl - 1)
    t = rng.choice(np.array([0, 1, 16, 31, 32]), (N, 8, 1, L))
    v = np.where(np.argsort(rng.random(v.shape), axis=2) < 2, t, np.minimum(rng.integers(0, 33, v.shape), t))
    return pack(x, c, p, a, v)
def setup_inputs_ends(rng):
    x, c, p, a, v = parts(rng)
    x = 15 * rng.integers(0, 2, x.shape); x[..., 0] = 0; x[..., W - 1] = 15
    e = rng.choice(np.array([0, 1, W // 2, W - 2, W - 1]), c.shape); c = np.where(rng.random((N, 8, 1, L, 1)) < 0.5, e, c)
    T = np.arange(16).reshape(1, 1, 16, 1, 1); k = rng.integers(0, 6, (N, 8, 1, L, 1))
    q = np.where(k == 0, T, np.where(k == 1, np.maximum(T - 1, 0), np.where(k == 2, 0, np.where(k == 3, 15, (T + 1) % 16))))
    p = np.where(k == 5, rng.integers(0, 16, p.shape), q)
    k = np.argsort(rng.random((N, 8, 1, L)), axis=-1) % 5; pos = np.argsort(rng.random(a.shape), axis=2)
    a = np.where(k == 0, 0, np.where(k == 1, 15, np.where(k == 2, 14, np.where(pos < np.where(k == 3, NEED, NEED - 1), 15, 0))))
    o = np.arange(OR).reshape(1, 1, OR, 1); k = rng.integers(0, 5, (N, 8, 1, L))
    v = np.where(k == 0, 0, np.where(k == 1, 32, np.where(k == 2, 32 * (o == 0), np.where(k == 3, 32 * (o == OR - 1), v))))
    z = int(rng.integers(0, 8)); w = np.argsort(rng.random(L)) % 4; x[:, z] = 15 * (np.arange(W) & 1)
    tt = T[0]; ring = (w == 0).reshape(1, 1, L, 1); climb = (w == 1).reshape(1, 1, L, 1)
    par = rng.integers(0, 2, (N, 1, L, OR)); even = c[:, z] - (c[:, z] & 1)
    c[:, z] = np.where(ring, even + ((par + tt) & 1), np.where(climb, even + ((par + (tt == 15)) & 1), c[:, z]))
    p[:, z] = np.where(ring, (tt + 1) % 16, np.where(climb, 0, p[:, z]))
    a = np.where(w == 1, 15, a); a[:, z] = np.where(w <= 1, 14 * rng.integers(0, 2, (N, 16, L)), a[:, z])
    v[:, z] = np.where(w == 1, 32 * (o[0] < 5) - 1 * (o[0] == 3), v[:, z])
    return pack(x, c, p, a, v)
def setup_inputs_alike(rng):
    x, c, p, a, v = parts(rng)
    x[:, ::2] = x[:, ::2][..., rng.integers(0, 8, W)]
    few = rng.integers(0, W, 5); few[0] = 0; few[1] = W - 1; c = few[rng.integers(0, 5, c.shape)]
    m = (rng.random((N, 8, 1, L, 1)) < 0.3) | (rng.random((N, 1, 1, L, 1)) < 0.3)
    c = np.where(m, c[:, :, :1], c); a[:, rng.integers(0, 8)] = 0
    return pack(x, c, p, a, v)
def setup_inputs_same(rng):
    x, c, p, a, v = parts(rng)
    o = np.arange(OR).reshape(1, 1, OR, 1); fav = rng.integers(0, OR, (1, 8, 1, L))
    v = np.where(o == fav, 32, rng.integers(0, 3, v.shape)); a = limits(rng, 5, 6)
    a[:, rng.integers(0, 8)] = rng.integers(0, 5, (N, 16, L))
    return pack(x, c, p, a, v)
def setup_inputs_spread(rng):
    x, c, p, a, v = parts(rng); E = np.array([0.25, 0.5, 1.0, 2.0, 4.0])
    def un(n, shape, by): return np.minimum((n * rng.random(shape) ** rng.choice(E, by)).astype(np.int64), n - 1)
    x = un(16, x.shape, (N, 8, 16, 1)); c = un(W, c.shape, (N, 8, 1, L, OR)); a = un(16, a.shape, (N, 8, 1, L)); v = un(33, v.shape, (N, 8, OR, 1))
    return pack(x, c, p, a, v)
def check_inputs(d):
    bad = []
    for k, hi in (("xt", 15), ("pg", W - 1), ("pre", 15), ("lim", 15), ("vv", 32)):
        b = np.asarray(d[k]).astype(np.float64)
        if not (np.min(b) >= 0 and np.max(b) <= hi and np.all(b == np.floor(b))): bad.append("range of " + k)
    return bad
def reference(xt, pg, pre, lim, vv):
    xs = np.ascontiguousarray(xt.astype(np.int32).reshape(N, 8, 16, W).transpose(0, 1, 3, 2))
    cur = np.ascontiguousarray(pg.astype(np.int64).reshape(N, 8, 16, L, OR).transpose(0, 1, 3, 4, 2))
    prd = np.ascontiguousarray(pre.astype(np.int64).reshape(N, 8, 16, L, OR).transpose(0, 1, 3, 4, 2))
    a = np.ascontiguousarray(lim.astype(np.int32).reshape(N, 8, 16, L).transpose(0, 1, 3, 2))
    v = np.ascontiguousarray(vv.astype(np.int64).reshape(N, 8, OR, L).transpose(0, 1, 3, 2))
    m = np.zeros((N, 8, L), np.int64)
    g0 = np.arange(8).reshape(1, 8, 1); l0 = np.arange(L).reshape(1, 1, L)
    for s in range(N):
        h = ((np.arange(N) + s) % N).reshape(N, 1, 1)
        o = np.argmax(v, axis=3)
        c = cur[h, g0, l0, o]; p = prd[h, g0, l0, o]
        got = np.zeros((N, 8, L), np.int64)
        for t in range(ST):
            F = xs[h[..., None], g0[..., None], c]
            G = np.take_along_axis(F, p[..., None], 3)
            D = np.abs(F - G)
            ok = np.add.reduce((D <= a[:, :, :, None, :]).astype(np.int64), axis=4) >= NEED
            full = np.all(ok, axis=3)
            got = got + full
            c = np.where(full[..., None], (5 * c + 1) & (W - 1), np.where(ok, c, (5 * c + np.add.reduce(D, axis=4) + 1) & (W - 1)))
        cur[h, g0, l0, o] = c
        m = m + got
        odd = np.add.reduce(got, axis=1, keepdims=True) & 1
        v = v + 1 + odd[..., None]
        np.put_along_axis(v, o[..., None], np.add.reduce(ok.astype(np.int64), axis=3)[..., None], 3)
    return {"yg": np.ascontiguousarray(cur.transpose(0, 1, 4, 2, 3)).reshape(N, 128, L * OR).astype(np.float32),
            "yv": np.ascontiguousarray(v.transpose(0, 1, 3, 2)).reshape(N, 8 * OR, L).astype(np.float32), "ym": m.astype(np.float32)}

from concourse.mybir import AluOpType, ActivationFunctionType

OP, AF = AluOpType, ActivationFunctionType
NCH, CN, NB = 4, 64, 4
SUB, HW = 2, 32
NSL, NST = 4, 3
BIG = 2 ** 17
HPW = 40
TB = 512 // NCH

PER = {"PGI": (256, "int32"), "PGB": (256, "int32"), "PRE": (256, "bfloat16"), "PW0": (256, "int32"), "PW": (256, "int32"), "CW": (256, "int32"),
       "VI": (16, "int32"), "VB": (16, "bfloat16"), "KS": (28, "float32"), "KM": (20, "float32"), "KN": (16, "int32"), "LI": (4, "int32"), "LU": (4, "uint16"),
       "E": (16, "bfloat16"), "EN": (16, "bfloat16"), "CB": (64, "int32"), "OFF": (64, "uint16"), "C16": (64, "float16"), "PO": (64, "uint16"),
       "O1": (64, "int32"), "O2": (64, "int32"), "NS": (192, "bfloat16"), "FM": (12, "bfloat16"), "CNT": (4, "bfloat16"), "MI": (4, "int32"), "OD": (4, "bfloat16"),
       "OUTF": (256, "float32"), "YV": (16, "float32"), "YM": (4, "float32"), "F": (1024, "bfloat16"), "F2": (1024, "bfloat16"), "D": (1024, "bfloat16"),
       "C": (1024, "bfloat16"), "HP": (HPW * NSL, "bfloat16"), "HL": (HPW * NSL, "bfloat16")}
ONE = {"XB": (2064, "bfloat16"), "LIM": (256, "bfloat16"), "LIMP": (256, "bfloat16"), "LS1": (256, "bfloat16"), "LS2": (256, "bfloat16"), "LS3": (256, "bfloat16"),
       "ONES": (128, "bfloat16"), "BO": (128, "bfloat16"), "BO0": (128, "bfloat16"), "ID": (128, "bfloat16"), "WB": (144, "bfloat16"), "RI": (128, "int32"),
       "RH": (128, "bfloat16"), "BIGI": (128, "bfloat16"), "NBO": (128, "bfloat16"), "IM64": (128, "bfloat16"), "IM32": (128, "bfloat16"), "IMV": (128, "bfloat16"),
       "I16": (128, "float16"), "I5": (128, "float16"), "BI": (16, "int32"), "B16": (16, "float16")}
SCRATCH = {}
for _n in PER:
    SCRATCH[_n] = ("sbuf", [128, PER[_n][0] * NCH], PER[_n][1])
for _n in ONE:
    SCRATCH[_n] = ("sbuf", [128, ONE[_n][0]], ONE[_n][1])
for _n in ["lim", "tiny", "c0", "c1"] + ["ab%d" % _k for _k in range(NCH)]:
    SCRATCH["P_" + _n] = ("psum", [128, 512], "float32")
SEMAPHORES = ["v", "s", "t", "gc", "loc", "lh"] + ["ls%d" % _s for _s in range(1, NSL)]
SEMAPHORES += ["%s_%d_%d" % (_b, _k, _s) for _b in ("hr", "hl") for _k in range(NCH) for _s in range(NSL)]


def X(T, name, k, a=0, b=None, step=1):
    w = PER[name][0]
    return T[name][:, w * k + a:w * k + (w if b is None else b):step]


GA, TC, HOP, GC = 1.15, 0.5, 5000, 1000
SHORT, LAG, SEM = 150, 3000.0, 60.0
AMP, SEED = 1000.0, 984


def build():
    ops = []

    def op(q, fn, r=(), w=(), bank=None, cost=80.0, k=0, sem=None):
        ops.append({"q": q, "fn": fn, "r": list(r), "w": list(w), "bank": bank, "cost": cost, "k": k, "sem": sem, "i": len(ops)})

    def V(fn, r, w, n, k=0, bank=None):
        op("v", fn, r, w, bank, max(64, n) + 15, k)

    def S(fn, r, w, n, k=0, bank=None):
        op("s", fn, r, w, bank, max(64, n) + 40, k)

    def TE(fn, r, w, n, k=0, bank=None):
        op("t", fn, r, w, bank, n * TC, k)

    def dma(q, out, in_, r, w, cost=3000.0, k=0):
        sem = "d%d" % sum(1 for o in ops if o["q"] in ("qs", "qa"))
        if sem not in SEMAPHORES:
            SEMAPHORES.append(sem)
        op(q, (out, in_), r, w, None, cost, k, sem)

    for k in range(NCH):
        lo = CN * k
        for o in range(4):
            dma("qs" if o < 2 or k else "qa", lambda T, k=k, o=o: X(T, "VI", k, NB * o, NB * (o + 1)), lambda T, o=o, lo=lo: T.vv[o::4, lo:lo + CN], [], ["VI%d.%d" % (k, o)], 2500, k)
        dma("qa" if k else "qs", lambda T, k=k: X(T, "PGI", k), lambda T, lo=lo: T.pg[:, 4 * lo:4 * (lo + CN)], [], ["PGI%d" % k], 3500, k)
        dma("qa", lambda T, k=k: X(T, "PRE", k), lambda T, lo=lo: T.pre[:, 4 * lo:4 * (lo + CN)], [], ["PRE%d" % k], 3500, k)
        if k == 0:
            dma("qs", lambda T: T.XB[:, 0:2048], lambda T: T.xt[:], [], ["XBa"], 6000, k)
            dma("qa", lambda T: T.XB[:, 2048:2064], lambda T: T.xt[:, 0:16], [], ["XBb"], 5000, k)
            dma("qa", lambda T: T.LIM[:], lambda T: T.lim[:], [], ["LIM"], 4500, k)
    op("g", lambda g, T: g.iota(T.BI[:], [[1, 4], [4, NB]], 0, 4 * NB), [], ["BI"], None, 250)
    V(lambda g, T: g.vector.memset(T.ONES[:], 1.0), [], ["ONES"], 128)
    V(lambda g, T: g.vector.memset(T.WB[:], 0.0), [], ["WB"], 144)
    op("g", lambda g, T: g.affine_select(T.ID[:], T.ONES[:], [[-1, 128]], OP.is_equal, 0.0, 0, 1), ["ONES"], ["ID"], None, 500)
    op("g", lambda g, T: g.iota(X(T, "PW0", 0), [[16, 16], [256, NB], [0, 4]], 0, 0), [], ["PW0"], None, 700)
    op("g", lambda g, T: g.affine_select(T.BO0[:], T.ONES[:], [[-16, 8], [0, 16]], OP.is_ge, 0.0, 0, 1), ["ONES"], ["BO0"], None, 500)
    op("g", lambda g, T: g.affine_select(T.BO[:], T.BO0[:], [[16, 8], [0, 16]], OP.is_ge, 0.0, 15, -1), ["BO0"], ["BO"], None, 500)
    op("g", lambda g, T: g.iota(T.RI[:], [[1, 128]], 0, -1), [], ["RI"], None, 400)

    def scaled(name, src, f):
        V(lambda g, T: g.vector.tensor_scalar(T[name][:], T[src][:], float(f), None, OP.mult), [src], [name], 128)

    V(lambda g, T: g.vector.tensor_scalar(T.BI[:], T.BI[:], 4 * CN - 1, None, OP.bitwise_and), ["BI"], ["BI"], 16)
    V(lambda g, T: g.vector.tensor_copy(T.B16[:], T.BI[:]), ["BI"], ["B16"], 16)
    scaled("IMV", "ID", -4 * CN)
    scaled("I16", "ID", 1)
    V(lambda g, T: g.vector.tensor_scalar(X(T, "PW0", 0), X(T, "PW0", 0), 16 * HW - 1, None, OP.bitwise_and), ["PW0"], ["PW0"], 256)
    V(lambda g, T: g.vector.tensor_copy(T.WB[:, 15:143:16], T.BO[:, 0:128:16]), ["BO", "WB"], ["WBB"], 8)
    scaled("I5", "ID", 5)
    scaled("BIGI", "ID", BIG)
    scaled("NBO", "BO", -(BIG // 16))
    scaled("IM64", "ID", -64)
    scaled("IM32", "ID", -32)
    V(lambda g, T: g.vector.tensor_scalar(T.RI[:], T.RI[:], 15, None, OP.bitwise_and), ["RI"], ["RI"], 128)
    V(lambda g, T: g.vector.tensor_scalar(T.RH[:], T.RI[:], 0, 0.5, OP.is_equal, OP.mult), ["RI"], ["RH"], 128)
    for k in range(NCH):
        V(lambda g, T, k=k: g.vector.tensor_copy(X(T, "VB", k), X(T, "VI", k)), ["VI%d.%d" % (k, o) for o in range(4)], ["VB%d" % k], 32, k)
        V(lambda g, T, k=k: g.vector.tensor_scalar(X(T, "PGB", k), X(T, "PGI", k), BIG + 2047, None, OP.add), ["PGI%d" % k], ["PGB%d" % k], 256, k)
        V(lambda g, T, k=k: g.vector.tensor_scalar(X(T, "CW", k), X(T, "PGB", k), BIG | 2047, None, OP.bitwise_and), ["PGB%d" % k], ["CW%d" % k], 256, k)
        V(lambda g, T, k=k: g.vector.tensor_tensor(X(T, "PW", k), X(T, "PRE", k), X(T, "PW0", 0), OP.add), ["PRE%d" % k, "PW0"], ["PW%d" % k], 512, k)
        for c in range(NB):
            V(lambda g, T, k=k, c=c: g.vector.tensor_copy(T.LIMP[:, CN * k + 16 * c:CN * k + 16 * c + 16], T.LIM[:, CN * k + c:CN * k + CN:NB]),
              ["LIM"], ["LIMP%d.%d" % (k, c)], 16, k)
    op("g", "limsend", ["LIMP%d.%d" % (k, c) for k in range(NCH) for c in range(NB)], ["limsent"], None, 2000)
    for s in range(1, NSL):
        op("hop", "lim%d" % s, ["limsent"], ["LS%d" % s], None, 9000, 0, "ls%d" % s)
    for s in range(NSL):
        for k in range(NCH):
            one_slice(s, k, op, V, S, TE, dma)
    return ops


def one_slice(s, k, op, V, S, TE, dma):
    kt = lambda b: "%s%d" % (b, k)
    lo, tb = CN * k, TB * k
    ltags = ["LIMP%d.%d" % (k, c) for c in range(NB)] if s == 0 else ["LS%d" % s]
    lname = "LIMP" if s == 0 else "LS%d" % s
    st = "HL%d.%d" % (k, s - 1)
    h0 = HPW * (s - 1)
    V4 = 4 * NB
    cb, ab = "c%d" % (k % 2), "ab%d" % k
    cc = CN * k

    def tiny(T, a, b):
        return T.P_tiny[:, tb + a:tb + b]

    def kmm(g, T):
        g.tensor.matmul(tiny(T, 0, V4), T.I16[:], T.B16[:], True, False)
        if s == 0:
            return g.tensor.matmul(tiny(T, 0, V4), T.IMV[:], X(T, "VB", k), False, True)
        g.tensor.matmul(tiny(T, 0, V4), T.IMV[:], X(T, "HL", k, h0, h0 + V4), False, False)
        return g.tensor.matmul(tiny(T, 0, V4), T.IMV[:], X(T, "HL", k, h0 + V4, h0 + 2 * V4), False, True)
    TE(kmm, ["IMV", "I16", "B16", st if s else kt("VB")], [kt("PSK")], 192, k, "tiny")
    S(lambda g, T: g.scalar.activation(X(T, "KS", k, 0, V4), tiny(T, 0, V4), AF.Copy), [kt("PSK")], [kt("KSa")], V4, k, "tiny")
    S(lambda g, T: g.scalar.activation(X(T, "KS", k, V4, 7 * NB), tiny(T, 0, 3 * NB), AF.Copy), [kt("PSK")], [kt("KSb")], V4, k, "tiny")
    V(lambda g, T: g.vector.tensor_tensor(X(T, "KM", k), X(T, "KS", k, 0, 5 * NB), X(T, "KS", k, 2 * NB, 7 * NB), OP.min), [kt("KSa"), kt("KSb")], [kt("KM")], 40, k)
    V(lambda g, T: g.vector.tensor_tensor(X(T, "KN", k), X(T, "KM", k, 0, V4), X(T, "KM", k, NB, 5 * NB), OP.min), [kt("KM")], [kt("KN")], 32, k)
    V(lambda g, T: g.vector.tensor_scalar(X(T, "LI", k), X(T, "KN", k, 0, NB), 4 * CN - 1, None, OP.bitwise_and), [kt("KN")], [kt("LI")], NB, k)
    V(lambda g, T: g.vector.tensor_copy(X(T, "LU", k), X(T, "LI", k)), [kt("LI")], [kt("LU")], NB, k)
    V(lambda g, T: g.vector.tensor_copy(X(T, "CB", k), X(T, "CW", k).indirect(X(T, "LU", k))), [kt("CW"), kt("LU")], [kt("CB")], GA * CN + 60, k)
    V(lambda g, T: g.vector.tensor_scalar(X(T, "OFF", k), X(T, "CB", k), 1 - BIG, None, OP.add), [kt("CB")], [kt("OFF")], CN, k)
    V(lambda g, T: g.vector.tensor_copy(X(T, "PO", k), X(T, "PW", k).indirect(X(T, "LU", k))), [kt("PW"), kt("LU")], [kt("PO")], GA * CN + 60, k)
    V(lambda g, T: g.vector.tensor_scalar(X(T, "C16", k), X(T, "CB", k), 1 - BIG, None, OP.add), [kt("CB")], [kt("C16")], CN, k)
    for e in range(2):
        V(lambda g, T, e=e: g.vector.tensor_copy(T.P_lim[:, 2 * lo + e:2 * (lo + CN):2], T[lname][:, lo:lo + CN]), ltags, ["PL%d.%d" % (k, e)], CN, k, "lim")
    V(lambda g, T: g.vector.tensor_tensor(X(T, "E", k), X(T, "KS", k, 0, V4), X(T, "KN", k), OP.is_equal), [kt("KSa"), kt("KN")], [kt("E")], 32, k)
    S(lambda g, T: g.scalar.activation(X(T, "EN", k), X(T, "E", k), AF.Identity, bias=1.0, scale=-1.0), [kt("E")], [kt("EN")], V4, k)

    for t in range(NST):
        last_step = s == NSL - 1 and t == NST - 1
        for u in range(SUB):
            f0, f1, y0, y1 = 16 * HW * u, 16 * HW * (u + 1), HW * u, HW * (u + 1)
            fu, gu = "F%d.%d" % (k, u), "G%d.%d" % (k, u)
            S(lambda g, T, y0=y0, y1=y1, f0=f0, f1=f1: g.scalar.activation(X(T, "F", k, f0, f1), T.XB[:].indirect(X(T, "OFF", k, y0, y1)), AF.Copy),
              ["XBa", "XBb", kt("OFF")], [fu], GA * 16 * HW + 25, k)
            op("g", lambda g, T, f0=f0, f1=f1: g.affine_select(X(T, "F2", k, f0, f1), X(T, "F", k, f0, f1), [[0, 16 * HW]], OP.is_ge, 0.0, 0, 0), [fu], [gu], None, GC, k)
        for u in range(SUB):
            f0, f1, y0, y1 = 16 * HW * u, 16 * HW * (u + 1), HW * u, HW * (u + 1)
            fu, gu, du, cu = "F%d.%d" % (k, u), "G%d.%d" % (k, u), "D%d.%d" % (k, u), "C%d.%d" % (k, u)
            V(lambda g, T, y0=y0, y1=y1, f0=f0, f1=f1: g.vector.tensor_tensor(X(T, "D", k, f0, f1), X(T, "F", k, f0, f1).indirect(X(T, "PO", k, y0, y1)), X(T, "F2", k, f0, f1), OP.subtract),
              [fu, gu, kt("PO")], [du], GA * 16 * HW + 35, k)
            S(lambda g, T, f0=f0, f1=f1: g.scalar.activation(X(T, "D", k, f0, f1), X(T, "D", k, f0, f1), AF.Abs), [du], [du], 16 * HW, k)

            def cmp(g, T, u=u, f0=f0, f1=f1):
                for q in range(8):
                    c0 = 2 * CN * q + 2 * HW * u
                    last = g.vector.tensor_tensor(X(T, "C", k, c0, c0 + 2 * HW), X(T, "D", k, f0 + q, f1, 8), T.P_lim[:, 2 * (lo + HW * u):2 * (lo + HW * (u + 1))], OP.is_gt)
                return last
            V(cmp, [du, "PL%d.0" % k, "PL%d.1" % k], [cu], 16 * HW, k, "lim")
        dts, cts = ["D%d.%d" % (k, u) for u in range(SUB)], ["C%d.%d" % (k, u) for u in range(SUB)]

        def ssum(g, T):
            A = T["P_" + ab][:, 0:CN]
            g.tensor.matmul(A, T.I5[:], X(T, "C16", k), True, False)
            for a in range(16):
                last = g.tensor.matmul(A, T.WB[:, 15 - a:143 - a], X(T, "D", k, a, None, 16), False, False)
            return last
        TE(ssum, dts + ["WBB", "I5", kt("C16")], [kt("PA")], 17 * CN, k, ab)

        def csum(g, T):
            A = T["P_" + cb][:, cc:cc + CN]
            for a in range(16):
                c0 = 2 * CN * (a % 8)
                last = g.tensor.matmul(A, T.WB[:, 15 - a:143 - a], X(T, "C", k, c0 + a // 8, c0 + 2 * CN, 2), a == 0, a == 15)
            return last
        TE(csum, cts + ["WBB"], [kt("PC")], 16 * CN, k, cb)
        S(lambda g, T, t=t: g.scalar.activation(X(T, "NS", k, CN * t, CN * (t + 1)), T["P_" + cb][:, cc:cc + CN], AF.Sign, bias=-7.5),
          [kt("PC")], ["NS%d.%d" % (k, t)], CN, k, cb)

        def absum(g, T, t=t):
            s_ = X(T, "NS", k, CN * t, CN * (t + 1))
            g.tensor.matmul(T["P_" + ab][:, 0:CN], T.BIGI[:], s_, False, True)
            g.tensor.matmul(T["P_" + ab][:, CN:2 * CN], T.I5[:], X(T, "C16", k), True, False)
            return g.tensor.matmul(T["P_" + ab][:, CN:2 * CN], T.NBO[:], s_, False, True)
        TE(absum, ["NS%d.%d" % (k, t), "BIGI", "I5", "NBO", kt("C16"), kt("PA")], [kt("PA"), kt("PB")], 3 * CN, k, ab)
        V(lambda g, T: g.vector.tensor_tensor(X(T, "O1", k), T["P_" + ab][:, 0:CN], X(T, "CB", k), OP.max), [kt("PA"), kt("CB")], [kt("O1")], CN, k, ab)
        V(lambda g, T: g.vector.tensor_tensor(X(T, "O2", k), T["P_" + ab][:, CN:2 * CN], X(T, "O1", k), OP.max), [kt("PB"), kt("O1")], [kt("O2")], CN, k, ab)
        if last_step:
            V(lambda g, T: g.vector.tensor_scalar(X(T, "O1", k), X(T, "O2", k), 1, None, OP.add), [kt("O2")], [kt("O1")], CN, k)
            V(lambda g, T: g.vector.tensor_scalar(X(T, "CB", k), X(T, "O1", k), 2047, None, OP.bitwise_and), [kt("O1")], [kt("CB")], CN, k)
        else:
            V(lambda g, T: g.vector.tensor_scalar(X(T, "CB", k), X(T, "O2", k), BIG | 2047, None, OP.bitwise_and), [kt("O2")], [kt("CB")], CN, k)
        if t < NST - 1:
            V(lambda g, T: g.vector.tensor_scalar(X(T, "OFF", k), X(T, "CB", k), 1 - BIG, None, OP.add), [kt("CB")], [kt("OFF")], CN, k)
            V(lambda g, T: g.vector.tensor_scalar(X(T, "C16", k), X(T, "CB", k), 1 - BIG, None, OP.add), [kt("CB")], [kt("C16")], CN, k)

    PN, PM, PX = V4, 7 * NB, 8 * NB

    def nsum(g, T):
        for a in range(16):
            last = g.tensor.matmul(tiny(T, PN, PN + 3 * NB), T.WB[:, 15 - a:143 - a], X(T, "NS", k, a, None, 16), a == 0, a == 15)
        return last
    TE(nsum, ["NS%d.%d" % (k, t) for t in range(NST)] + ["WBB"], [kt("PN")], 1024, k, "tiny")
    S(lambda g, T: g.scalar.activation(X(T, "FM", k), tiny(T, PN, PN + 3 * NB), AF.Relu, bias=-15.0, scale=-1.0), [kt("PN")], [kt("FM")], 3 * NB, k, "tiny")
    S(lambda g, T: g.scalar.activation(X(T, "CNT", k), tiny(T, PN + 2 * NB, PN + 3 * NB), AF.Identity, bias=8.0, scale=-0.5), [kt("PN")], [kt("CNT")], NB, k, "tiny")

    def msum(g, T):
        for t in range(NST):
            last = g.tensor.matmul(tiny(T, PM, PM + NB), T.RH[:], X(T, "FM", k, t * NB, (t + 1) * NB), t == 0, t == NST - 1)
        return last
    TE(msum, [kt("FM"), "RH"], [kt("PM")], 192, k, "tiny")
    V(lambda g, T: g.vector.tensor_copy(X(T, "MI", k), tiny(T, PM, PM + NB)), [kt("PM")], [kt("MI")], NB, k, "tiny")
    V(lambda g, T: g.vector.tensor_tensor(X(T, "OD", k), tiny(T, PM, PM + NB), X(T, "MI", k), OP.not_equal), [kt("PM"), kt("MI")], [kt("OD")], NB, k, "tiny")

    def bsum(g, T):
        B = tiny(T, PX + V4, PX + 2 * V4)
        g.tensor.matmul(B, T.IM32[:], X(T, "EN", k), True, False)
        for o in range(4):
            g.tensor.matmul(tiny(T, PX + V4 + o * NB, PX + V4 + (o + 1) * NB), T.ID[:], X(T, "CNT", k), False, False)
        g.tensor.matmul(B, T.IM32[:], X(T, "EN", k), False, True)
        M = tiny(T, PX + 2 * V4, PX + 2 * V4 + NB)
        for t in range(NST):
            last = g.tensor.matmul(M, T.ID[:], X(T, "FM", k, t * NB, (t + 1) * NB), t == 0, t == NST - 1 and s == 0)
        if s > 0:
            last = g.tensor.matmul(M, T.ID[:], X(T, "HL", k, h0 + 2 * V4, h0 + 2 * V4 + NB), False, True)
        return last
    TE(bsum, [kt("EN"), kt("CNT"), kt("FM"), "IM32", "ID"] + ([st] if s else []), [kt("PX")], 640, k, "tiny")

    def asum(g, T):
        A = tiny(T, PX, PX + V4)
        if s == 0:
            g.tensor.matmul(A, T.ID[:], X(T, "VB", k), True, False)
        else:
            g.tensor.matmul(A, T.ID[:], X(T, "HL", k, h0, h0 + V4), True, False)
            g.tensor.matmul(A, T.ID[:], X(T, "HL", k, h0 + V4, h0 + 2 * V4), False, False)
        g.tensor.matmul(A, T.ID[:], X(T, "EN", k), False, False)
        for o in range(4):
            g.tensor.matmul(tiny(T, PX + o * NB, PX + (o + 1) * NB), T.ID[:], X(T, "OD", k), False, False)
        return g.tensor.matmul(A, T.IM64[:], X(T, "E", k), False, True)
    TE(asum, [kt("E"), kt("EN"), kt("OD"), "IM64", "ID", st if s else kt("VB")], [kt("PY")], 512, k, "tiny")
    hp, hl = "HP%d.%d" % (k, s), "HL%d.%d" % (k, s)
    g0 = HPW * s
    S(lambda g, T: g.scalar.activation(X(T, "HP", k, g0, g0 + 9 * NB), tiny(T, PX, PX + 9 * NB), AF.Relu), [kt("PX"), kt("PY")], [hp], 9 * NB, k, "tiny")
    op("g", ("send", k, s), [hp], ["snt%d.%d" % (k, s)], None, 1000, k)
    op("hop", "hop", ["snt%d.%d" % (k, s)], [hl], None, HOP, k, "hl_%d_%d" % (k, s))
    if s < NSL - 1:
        V(lambda g, T: g.vector.tensor_copy(X(T, "CW", k).indirect(X(T, "LU", k)), X(T, "CB", k)), [kt("CB"), kt("LU")], [kt("CW")], 4 * CN + 60, k)
    if s == NSL - 2:
        V(lambda g, T: g.vector.tensor_scalar(X(T, "PGB", k), X(T, "CW", k), 1, None, OP.add), [kt("CW")], [kt("PGB")], 256, k)
        V(lambda g, T: g.vector.tensor_scalar(X(T, "PGI", k), X(T, "PGB", k), 2047, None, OP.bitwise_and), [kt("PGB")], [kt("PGI")], 256, k)
        V(lambda g, T: g.vector.tensor_copy(X(T, "OUTF", k), X(T, "PGI", k)), [kt("PGI")], [kt("OUTF")], 256, k)
    if s == NSL - 1:
        V(lambda g, T: g.vector.tensor_copy(X(T, "OUTF", k).indirect(X(T, "LU", k)), X(T, "CB", k)), [kt("CB"), kt("LU"), kt("OUTF")], [kt("OUTF")], 4 * CN + 60, k)
        dma("qs", lambda T: T.yg[:, 4 * lo:4 * (lo + CN)], lambda T: X(T, "OUTF", k), [kt("OUTF")], [], 3500, k)
        V(lambda g, T: g.vector.tensor_tensor(X(T, "YV", k), X(T, "HL", k, g0, g0 + V4), X(T, "HL", k, g0 + V4, g0 + 2 * V4), OP.add), [hl], [kt("YV")], 32, k)
        S(lambda g, T: g.scalar.activation(X(T, "YM", k), X(T, "HL", k, g0 + 2 * V4, g0 + 2 * V4 + NB), AF.Copy), [hl], [kt("YM")], NB, k)
        for o in range(4):
            dma("qs", lambda T, o=o: T.yv[o::4, lo:lo + CN], lambda T, o=o: X(T, "YV", k, NB * o, NB * (o + 1)), [kt("YV")], [], 2500, k)
        dma("qs", lambda T: T.ym[:, lo:lo + CN], lambda T: X(T, "YM", k), [kt("YM")], [], 2500, k)


def jitter(n):
    x, out = SEED, []
    for _ in range(n):
        x = (x * 1103515245 + 12345) % 2 ** 31
        out.append(AMP * (x / 2 ** 31 - 0.5))
    return out


def plan(ops):
    n = len(ops)
    lastw, readers = {}, {}
    deps = [set() for _ in range(n)]
    for o in ops:
        i = o["i"]
        for r in o["r"]:
            if r in lastw:
                deps[i].add(lastw[r])
        for w in o["w"]:
            if w in lastw:
                deps[i].add(lastw[w])
            deps[i].update(readers.get(w, ()))
        for r in o["r"]:
            readers.setdefault(r, set()).add(i)
        for w in o["w"]:
            lastw[w] = i
            readers[w] = set()
        deps[i].discard(i)
    succ = [[] for _ in range(n)]
    for i in range(n):
        for d in deps[i]:
            succ[d].append(i)
    tail = [0.0] * n
    for i in range(n - 1, -1, -1):
        tail[i] = ops[i]["cost"] + max([tail[j] + SEM for j in succ[i]] + [0.0])
    nz = jitter(n)
    prio = [tail[i] - LAG * ops[i]["k"] + nz[i] for i in range(n)]
    left = [len(d) for d in deps]
    ready_at, fin = [0.0] * n, [0.0] * n
    free, bankfree, bankq = {}, {}, {}
    avail = [i for i in range(n) if left[i] == 0]
    order = []
    while len(order) < n:
        best = None
        for i in avail:
            o = ops[i]
            at = ready_at[i]
            if o["q"] != "hop":
                at = max(at, free.get(o["q"], 0.0))
            b = o["bank"]
            if b and bankq.get(b) not in (None, o["q"]):
                at = max(at, bankfree[b] + SEM)
            key = (at, o["cost"] > SHORT, -prio[i], i)
            if best is None or key < best:
                best = key
        i, at = best[3], best[0]
        o = ops[i]
        avail.remove(i)
        fin[i] = at + o["cost"]
        if o["q"] != "hop":
            free[o["q"]] = (at + 120) if o["q"] in ("qs", "qa") else fin[i]
        if o["bank"]:
            bankq[o["bank"]] = o["q"]
            bankfree[o["bank"]] = fin[i]
        order.append(i)
        for j in succ[i]:
            left[j] -= 1
            ready_at[j] = max(ready_at[j], fin[i] + SEM)
            if left[j] == 0:
                avail.append(j)
    return order, deps, fin


_PLAN = []


def get_plan():
    if not _PLAN:
        ops = build()
        order, deps, fin = plan(ops)
        _PLAN.extend([ops, order, deps, fin])
    return _PLAN


get_plan()


def helpers(topo, core, nxt, group):
    return [c for c in topo.cores_of(core) if c not in group and topo.die(c) == topo.die(core) and topo.may_write(c, nxt)]


def bits(topo, a, b):
    return len(topo.engines(a, b))


def rank_program(g, core, T, topo):
    cores = list(T.cores)
    n = len(cores)
    rank = T.rank_of(core)
    if rank is not None:
        run_rank(g, core, T, topo, cores, rank)
        return
    for r in range(n):
        own, nxt, prv = cores[r], cores[(r + 1) % n], cores[(r + 3) % n]
        hs = helpers(topo, own, nxt, cores)
        if core in hs:
            hand_on(g, core, T, topo, own, nxt, prv, [k for k in range(NCH) if hs[k % len(hs)] == core], hs[0] == core)


def hand_on(g, core, T, topo, own, nxt, prv, ks, lims):
    loc = 0

    def remote(out, in_, sem, dst):
        rid, pid = topo.addr(dst, core)
        g.remote_dma(out, in_, T.sem[sem], T.sem.loc, pid, rid, topo.mask(core, dst))
        return bits(topo, core, dst)

    if lims:
        g.wait_ge(T.sem.lh, bits(topo, own, core))
        loc += remote(T.LS1[:], T.LIMP[:], "ls1", nxt)
        loc += remote(T.LS3[:], T.LIMP[:], "ls3", prv)
    for s in range(NSL):
        for k in ks:
            g.wait_ge(T.sem["hr_%d_%d" % (k, s)], bits(topo, own, core))
            a, b = HPW * s, HPW * s + 9 * NB
            loc += remote(X(T, "HL", k, a, b), X(T, "HP", k, a, b), "hl_%d_%d" % (k, s), nxt)
    if loc:
        g.wait_ge(T.sem.loc, loc)


def run_rank(g, core, T, topo, cores, rank):
    n = len(cores)
    nxt, opp, prv = cores[(rank + 1) % n], cores[(rank + 2) % n], cores[(rank + 3) % n]
    hs, hprev, hnext = helpers(topo, core, nxt, cores), helpers(topo, prv, core, cores), helpers(topo, nxt, opp, cores)
    ops, order, deps, _f = get_plan()
    eng = {"v": g.vector, "s": g.scalar, "t": g.tensor, "g": g, "qs": g.sync, "qa": g.scalar}
    semname = {"v": "v", "s": "s", "t": "t", "g": "gc"}
    count = {"v": 0, "s": 0, "t": 0, "g": 0}
    done, waited, banks, loc = {}, {}, {}, [0]

    def queue(q):
        return "s" if q == "qa" else q

    def wait(q, d):
        if d in done:
            sem, val = done[d]
            key = (queue(q), sem)
            if waited.get(key, 0) < val:
                eng[q].wait_ge(T.sem[sem], val)
                waited[key] = val

    def remote(out, in_, sem, dst):
        rid, pid = topo.addr(dst, core)
        g.remote_dma(out, in_, T.sem[sem], T.sem.loc, pid, rid, topo.mask(core, dst))
        loc[0] += bits(topo, core, dst)

    for i in order:
        o = ops[i]
        q = o["q"]
        if q == "hop":
            src = hprev[o["k"] % len(hprev)] if o["fn"] == "hop" else {"ls1": hprev[0], "ls2": opp, "ls3": hnext[0]}[o["sem"]]
            done[i] = (o["sem"], bits(topo, src, core))
            continue
        for d in sorted(deps[i], reverse=True):
            if not (q == "t" and ops[d]["q"] == "t"):
                wait(q, d)
        if o["bank"]:
            for qq, d in banks.get(o["bank"], {}).items():
                if qq != q:
                    wait(q, d)
            banks.setdefault(o["bank"], {})[q] = i
        if q in ("qs", "qa"):
            out, in_ = o["fn"]
            eng[q].dma_start(out(T), in_(T)).then_inc(T.sem[o["sem"]], 16)
            done[i] = (o["sem"], 16)
        elif o["fn"] == "limsend":
            remote(T.LIMP[:], T.LIMP[:], "lh", hs[0])
            remote(T.LS2[:], T.LIMP[:], "ls2", opp)
        elif q == "g" and isinstance(o["fn"], tuple):
            _x, k, s = o["fn"]
            a, b = HPW * s, HPW * s + 9 * NB
            remote(X(T, "HP", k, a, b), X(T, "HP", k, a, b), "hr_%d_%d" % (k, s), hs[k % len(hs)])
        else:
            ins = o["fn"](g, T)
            count[q] += 1
            ins.then_inc(T.sem[semname[q]], 1)
            done[i] = (semname[q], count[q])
    for q in ("v", "s", "t", "g"):
        g.wait_ge(T.sem[semname[q]], count[q])
    g.wait_ge(T.sem.loc, loc[0])
    for o in ops:
        if o["q"] in ("qs", "qa"):
            g.wait_ge(T.sem[o["sem"]], 16)
